import numpy as np
import ml_dtypes


def mxq(x, axis, fmt="e4m3"):
    dtype, down = {"e4m3": (ml_dtypes.float8_e4m3fn, 7), "e5m2": (ml_dtypes.float8_e5m2, 14)}[fmt]
    v = np.moveaxis(np.asarray(x, np.float32).astype(ml_dtypes.bfloat16).astype(np.float64), axis, -1)
    blocks = v.reshape(v.shape[:-1] + (-1, 32))
    amax = np.abs(blocks).max(-1, keepdims=True)
    byte = np.maximum(np.where(amax > 0, np.frexp(amax)[1] - 1 + 127, 0) - down, 1)
    scale = np.exp2(byte - 127.0)
    codes = (blocks / scale).astype(np.float32).astype(dtype).astype(np.float64)
    return np.moveaxis((codes * scale).reshape(v.shape), -1, axis)


WIDE = False


def mx_kscale(k):
    if not WIDE:
        return np.ones(k)
    levels = np.array([10, -10, 5, -5, 0])
    if k % 512:
        return np.exp2(np.random.permutation(np.resize(levels, k // 32))).repeat(32)
    a = np.empty((k // 512, 16))
    for p in range(k // 512):
        a[p, :8] = np.random.permutation(np.resize(levels, 8))
        for g in range(8):
            far = levels[np.abs(levels - a[p, g]) >= 10]
            a[p, g + 8] = far[np.random.randint(len(far))]
    return np.exp2(a.ravel()).repeat(32)


def f64(x):
    return np.asarray(x).astype(np.float64)


def striped8(idx):
    return np.concatenate([v.reshape(-1, 16).T for v in idx]).astype(np.uint16)


def unstriped8(offs):
    return np.stack([offs[16 * g:16 * g + 16].T.reshape(-1) for g in range(8)]).astype(np.int64)


E2M1 = np.array([0.0, 0.5, 1.0, 1.5, 2.0, 3.0, 4.0, 6.0, -0.0, -0.5, -1.0, -1.5, -2.0, -3.0, -4.0, -6.0])


def pack_weight(w, fmt):
    k, n = w.shape
    w = f64(np.asarray(w, np.float32).astype(ml_dtypes.bfloat16)).reshape(k // 32, 32, n)
    amax = np.abs(w).max(1)
    if fmt == "e4m3":
        byte = np.frexp(amax)[1] - 1 + 127 - 7
    else:
        mant, ex = np.frexp(amax / 6.0)
        byte = np.where(mant > 0.5, ex, ex - 1) + 127
    byte = np.clip(np.where(amax > 0, byte, 1), 1, 254)
    scaled = (w * np.exp2(127.0 - byte)[:, None, :]).reshape(k, n).astype(np.float32)
    by_word = np.ascontiguousarray(scaled.reshape(k // 512, 128, 4, n).transpose(0, 1, 3, 2))
    if fmt == "e4m3":
        words = by_word.astype(ml_dtypes.float8_e4m3fn).view(np.uint8)
    else:
        c = by_word.astype(ml_dtypes.float4_e2m1fn).view(np.uint8) & 0xF
        words = (c[..., 0::2] | (c[..., 1::2] << 4)).reshape(k // 512, 128, 2 * n)
    return np.ascontiguousarray(words), np.ascontiguousarray(byte.astype(np.uint8).reshape(k // 512, 16, n))


def unpack_weight(words, scales, fmt):
    g, _, n = scales.shape
    words = np.ascontiguousarray(words).reshape(g, 128, n, -1)
    if fmt == "e4m3":
        vals = words.view(ml_dtypes.float8_e4m3fn).astype(np.float64)
    else:
        nib = np.empty((g, 128, n, 4), np.uint8)
        nib[..., 0::2] = words & 0xF
        nib[..., 1::2] = words >> 4
        vals = E2M1[nib]
    vals = vals * np.repeat(np.exp2(scales.astype(np.float64) - 127.0), 8, axis=1)[..., None]
    return vals.transpose(0, 1, 3, 2).reshape(g * 512, n)


K, M, T, S = 512, 256, 1024, 512


def setup_inputs():
    n = np.random.standard_normal
    s = mx_kscale(K)[:, None]
    w = n((K, M)) / np.sqrt(K) / s
    w4 = pack_weight(w, "e2m1")
    rest = w - unpack_weight(*w4, "e2m1")
    p_r8 = pack_weight(rest, "e4m3")
    return {
        "xT": (n((K, T)) * s).astype(np.float32),
        "w4_words": w4[0],
        "w4_scales": w4[1],
        "r8_words": p_r8[0],
        "r8_scales": p_r8[1],
        "wgt": np.repeat(np.random.uniform(0.5, 2.0, (8, S)), 16, axis=0).astype(np.float32),
        "b": (0.3 * n(256)).astype(np.float32),
        "wgo": np.repeat(np.random.uniform(0.5, 2.0, (8, S)), 16, axis=0).astype(np.float32),
        "offs": striped8(np.stack([np.random.permutation(T)[:S] for _ in range(8)])),
        "offs2": striped8(np.stack([np.random.permutation(T)[:S] for _ in range(8)])),
    }


def reference(xT, w4_words, w4_scales, r8_words, r8_scales, wgt, b, wgo, offs, offs2):
    idx = unstriped8(offs)
    group = np.arange(K) % 512 // 64
    xg = f64(wgt)[np.arange(K) // 4 % 128] * f64(xT)[np.arange(K)[:, None], idx[group]]
    xT_ = mxq(xg, 0, "e4m3")
    w4_ = unpack_weight(w4_words, w4_scales, "e2m1")
    r8_ = unpack_weight(r8_words, r8_scales, "e4m3")
    y = w4_.T @ xT_ + r8_.T @ xT_
    place = unstriped8(offs2)[np.arange(M) % 128 // 16]
    out = np.zeros((M, T))
    out[np.arange(M)[:, None], place] = f64(wgo)[np.arange(M) % 128] * (y + f64(b)[:, None])
    return out

@@ -1,0 +1,165 @@
+from contextlib import ExitStack
+
+import concourse.mybir as mybir
+
+K, M, T, S = 512, 256, 1024, 512
+
+F32 = mybir.dt.float32
+BF16 = mybir.dt.bfloat16
+I32 = mybir.dt.int32
+U32 = mybir.dt.uint32
+U16 = mybir.dt.uint16
+U8 = mybir.dt.uint8
+E4M3X4 = mybir.dt.float8_e4m3fn_x4
+E2M1X4 = mybir.dt.float4_e2m1fn_x4
+MULT = mybir.AluOpType.mult
+COPY = mybir.ActivationFunctionType.Copy
+IDENTITY = mybir.ActivationFunctionType.Identity
+
+P = 128
+PACK = 4
+HALF = S // 2
+LIST_COLS = HALF // 16
+N_MM = 128
+FLOPS = 2 * 2 * K * M * S
+
+
+def tile_list_hboth_bias_kernel(
+    tc, xT, w4_words, w4_scales, r8_words, r8_scales, wgt, b, wgo, offs, offs2, out
+):
+    nc = tc.nc
+    with ExitStack() as ctx:
+        held = ctx.enter_context(tc.tile_pool(name="held", bufs=1))
+        psum = ctx.enter_context(tc.psum_pool(name="psum", bufs=1))
+
+        lists_in = held.tile([P, S // 16], U16, name="lists_in")
+        lists_out = held.tile([P, S // 16], U16, name="lists_out")
+        wgt_t = [held.tile([P, HALF], F32, name=f"wgt_t{c}") for c in range(2)]
+        wgo_t = held.tile([P, S], F32, name="wgo_t")
+        bias = held.tile([P, M // P], F32, name="bias")
+        planes = [held.tile([P, T], F32, name=f"plane{t}") for t in range(PACK)]
+        w4 = held.tile([P, 2 * M], U8, name="w4", align_bytes=64)
+        r8 = held.tile([P, 4 * M], U8, name="r8", align_bytes=64)
+        scales = held.tile([P, 2 * M], U8, name="scales", align_bytes=64)
+        windows = [held.tile([P, T], F32, name=f"window{m}") for m in range(M // P)]
+        picked = [held.tile([P, PACK, HALF], F32, name=f"picked{c}") for c in range(2)]
+        grouped = [held.tile([P, HALF, PACK], BF16, name=f"grouped{c}", align_bytes=64) for c in range(2)]
+        codes = [held.tile([P, HALF], U32, name=f"codes{c}", align_bytes=64) for c in range(2)]
+        xscales = [held.tile([P, HALF], U8, name=f"xscales{c}", align_bytes=64) for c in range(2)]
+        y = [[held.tile([P, HALF], F32, name=f"y{c}{m}") for m in range(M // P)] for c in range(2)]
+        acc = [
+            [[psum.tile([P, N_MM], F32, name=f"acc{c}{m}{h}") for h in range(2)] for m in range(M // P)]
+            for c in range(2)
+        ]
+
+        nc.vector.memset(scales[:].bitcast(I32), 0)
+        for m in range(M // P):
+            nc.vector.memset(windows[m][:], 0.0)
+
+        x_rows = xT.rearrange("(p j) w -> p j w", j=PACK)
+
+        def load_scales(queue, source, q, first):
+            queue.dma_start(
+                scales[32 * q : 32 * q + 4, first : first + M].bitcast(I32),
+                source[0, 4 * q : 4 * q + 4, :].bitcast(I32),
+            )
+
+        nc.sync.dma_start(lists_in[:], offs)
+        nc.sync.dma_start(wgt_t[0][:], wgt[:, 0:HALF])
+        nc.sync.dma_start(planes[0][:], x_rows[:, 0, :])
+        nc.sync.dma_start(wgt_t[1][:], wgt[:, HALF:S])
+        nc.sync.dma_start(planes[1][:], x_rows[:, 1, :])
+        for q in range(4):
+            load_scales(nc.sync, w4_scales, q, 0)
+        for q in range(3):
+            load_scales(nc.gpsimd, r8_scales, q, M)
+        nc.sync.dma_start(planes[2][:], x_rows[:, 2, :])
+        load_scales(nc.sync, r8_scales, 3, M)
+        nc.sync.dma_start(planes[3][:], x_rows[:, 3, :])
+        nc.sync.dma_start(r8[:].bitcast(I32), r8_words[0].rearrange("p n i -> p (n i)").bitcast(I32))
+        nc.sync.dma_start(w4[:].bitcast(I32), w4_words[0].bitcast(I32))
+        nc.sync.dma_start(wgo_t[:], wgo)
+        nc.sync.dma_start(lists_out[:], offs2)
+        with nc.allow_non_contiguous_dma(reason="one bias value to a partition"):
+            nc.sync.dma_start(bias[:], b.rearrange("(m p) -> p m", p=P))
+
+        def gather(t, c, lo=0, hi=HALF):
+            first = c * HALF + lo
+            nc.vector.tensor_tensor(
+                picked[c][:, t, lo:hi],
+                planes[t][:].indirect(lists_in[:, first // 16 : (first + hi - lo) // 16]),
+                wgt_t[c][:, lo:hi],
+                MULT,
+            )
+
+        def group(copy, c, t0, lo=0, hi=HALF):
+            copy(
+                grouped[c][:, lo:hi, t0 : t0 + 2],
+                picked[c][:, t0 : t0 + 2, lo:hi].rearrange("p t n -> p n t"),
+            )
+
+        def quantize(c, lo, hi):
+            nc.vector.quantize_mx(
+                out=codes[c][:, lo:hi].bitcast(E4M3X4),
+                scales=xscales[c][:, lo:hi],
+                in_=grouped[c][:, lo:hi, :].rearrange("p n t -> p (n t)"),
+            )
+
+        def multiply(c, m):
+            for h in range(2):
+                cols = slice(h * N_MM, (h + 1) * N_MM)
+                nc.tensor.matmul_mx(
+                    out=acc[c][m][h][:],
+                    lhsT=w4[:, 2 * m * P : 2 * (m + 1) * P].bitcast(E2M1X4),
+                    lhsT_scale=scales[:, m * P : (m + 1) * P],
+                    rhs=codes[c][:, cols].bitcast(E4M3X4),
+                    rhs_scale=xscales[c][:, cols],
+                    start=True,
+                    stop=False,
+                )
+                nc.tensor.matmul_mx(
+                    out=acc[c][m][h][:],
+                    lhsT=r8[:, 4 * m * P : 4 * (m + 1) * P].bitcast(E4M3X4),
+                    lhsT_scale=scales[:, M + m * P : M + (m + 1) * P],
+                    rhs=codes[c][:, cols].bitcast(E4M3X4),
+                    rhs_scale=xscales[c][:, cols],
+                    start=False,
+                    stop=True,
+                )
+                nc.scalar.activation(y[c][m][:, cols], acc[c][m][h][:], IDENTITY, bias=bias[:, m : m + 1], scale=1.0)
+
+        def scatter(c, m):
+            nc.vector.tensor_tensor(
+                windows[m][:].indirect(lists_out[:, c * LIST_COLS : (c + 1) * LIST_COLS]),
+                y[c][m][:],
+                wgo_t[:, c * HALF : (c + 1) * HALF],
+                MULT,
+            )
+
+        for t in range(2):
+            gather(t, 0)
+            gather(t, 1)
+        group(nc.scalar.copy, 0, 0)
+        group(nc.scalar.copy, 1, 0)
+        gather(2, 0)
+        gather(2, 1)
+        for h in range(2):
+            gather(3, 0, h * N_MM, (h + 1) * N_MM)
+        for h in range(2):
+            group(nc.scalar.copy, 0, 2, h * N_MM, (h + 1) * N_MM)
+        for h in range(2):
+            quantize(0, h * N_MM, (h + 1) * N_MM)
+        multiply(0, 0)
+        multiply(0, 1)
+        for h in range(2):
+            gather(3, 1, h * N_MM, (h + 1) * N_MM)
+        for h in range(2):
+            group(nc.scalar.copy, 1, 2, h * N_MM, (h + 1) * N_MM)
+        quantize(1, 0, HALF)
+        multiply(1, 0)
+        multiply(1, 1)
+        for c in range(2):
+            for m in range(M // P):
+                scatter(c, m)
+                if c == 1:
+                    nc.sync.dma_start(out[m * P : (m + 1) * P, :], windows[m][:])

@@ -69,13 +69,14 @@ def tile_list_hboth_bias_kernel(
         nc.sync.dma_start(planes[0][:], x_rows[:, 0, :])
         nc.sync.dma_start(wgt_t[1][:], wgt[:, HALF:S])
         nc.sync.dma_start(planes[1][:], x_rows[:, 1, :])
-        for q in range(4):
+        for q in range(3):
             load_scales(nc.sync, w4_scales, q, 0)
         for q in range(3):
             load_scales(nc.gpsimd, r8_scales, q, M)
         nc.sync.dma_start(planes[2][:], x_rows[:, 2, :])
-        load_scales(nc.sync, r8_scales, 3, M)
         nc.sync.dma_start(planes[3][:], x_rows[:, 3, :])
+        load_scales(nc.sync, w4_scales, 3, 0)
+        load_scales(nc.sync, r8_scales, 3, M)
         nc.sync.dma_start(r8[:].bitcast(I32), r8_words[0].rearrange("p n i -> p (n i)").bitcast(I32))
         nc.sync.dma_start(w4[:].bitcast(I32), w4_words[0].bitcast(I32))
         nc.sync.dma_start(wgo_t[:], wgo)
@@ -105,8 +106,8 @@ def tile_list_hboth_bias_kernel(
                 in_=grouped[c][:, lo:hi, :].rearrange("p n t -> p (n t)"),
             )
 
-        def multiply(c, m):
-            for h in range(2):
+        def multiply(c, m, halves=(0, 1)):
+            for h in halves:
                 cols = slice(h * N_MM, (h + 1) * N_MM)
                 nc.tensor.matmul_mx(
                     out=acc[c][m][h][:],
@@ -128,11 +129,12 @@ def tile_list_hboth_bias_kernel(
                 )
                 nc.scalar.activation(y[c][m][:, cols], acc[c][m][h][:], IDENTITY, bias=bias[:, m : m + 1], scale=1.0)
 
-        def scatter(c, m):
+        def scatter(c, m, lo=0, hi=HALF):
+            first = c * HALF + lo
             nc.vector.tensor_tensor(
-                windows[m][:].indirect(lists_out[:, c * LIST_COLS : (c + 1) * LIST_COLS]),
-                y[c][m][:],
-                wgo_t[:, c * HALF : (c + 1) * HALF],
+                windows[m][:].indirect(lists_out[:, first // 16 : (first + hi - lo) // 16]),
+                y[c][m][:, lo:hi],
+                wgo_t[:, first : first + hi - lo],
                 MULT,
             )
 
@@ -149,17 +151,19 @@ def tile_list_hboth_bias_kernel(
             group(nc.scalar.copy, 0, 2, h * N_MM, (h + 1) * N_MM)
         for h in range(2):
             quantize(0, h * N_MM, (h + 1) * N_MM)
-        multiply(0, 0)
+        multiply(0, 0, (0,))
         multiply(0, 1)
+        multiply(0, 0, (1,))
         for h in range(2):
             gather(3, 1, h * N_MM, (h + 1) * N_MM)
         for h in range(2):
             group(nc.scalar.copy, 1, 2, h * N_MM, (h + 1) * N_MM)
         quantize(1, 0, HALF)
-        multiply(1, 0)
         multiply(1, 1)
-        for c in range(2):
-            for m in range(M // P):
-                scatter(c, m)
-                if c == 1:
-                    nc.sync.dma_start(out[m * P : (m + 1) * P, :], windows[m][:])
+        multiply(1, 0)
+        scatter(0, 0, 0, N_MM)
+        scatter(0, 1)
+        scatter(0, 0, N_MM, HALF)
+        for m in (1, 0):
+            scatter(1, m)
+            nc.sync.dma_start(out[m * P : (m + 1) * P, :], windows[m][:])

@@ -34,7 +34,7 @@ def tile_list_hboth_bias_kernel(
 
         lists_in = held.tile([P, S // 16], U16, name="lists_in")
         lists_out = held.tile([P, S // 16], U16, name="lists_out")
-        wgt_t = [held.tile([P, HALF], F32, name=f"wgt_t{c}") for c in range(2)]
+        wgt_t = held.tile([P, S], F32, name="wgt_t")
         wgo_t = held.tile([P, S], F32, name="wgo_t")
         bias = held.tile([P, M // P], F32, name="bias")
         planes = [held.tile([P, T], F32, name=f"plane{t}") for t in range(PACK)]
@@ -42,7 +42,7 @@ def tile_list_hboth_bias_kernel(
         r8 = held.tile([P, 4 * M], U8, name="r8", align_bytes=64)
         scales = held.tile([P, 2 * M], U8, name="scales", align_bytes=64)
         windows = [held.tile([P, T], F32, name=f"window{m}") for m in range(M // P)]
-        picked = [held.tile([P, PACK, HALF], F32, name=f"picked{c}") for c in range(2)]
+        picked = [held.tile([P, 2, S], F32, name=f"picked{pair}") for pair in range(2)]
         grouped = [held.tile([P, HALF, PACK], BF16, name=f"grouped{c}", align_bytes=64) for c in range(2)]
         codes = [held.tile([P, HALF], U32, name=f"codes{c}", align_bytes=64) for c in range(2)]
         xscales = [held.tile([P, HALF], U8, name=f"xscales{c}", align_bytes=64) for c in range(2)]
@@ -54,7 +54,7 @@ def tile_list_hboth_bias_kernel(
 
         nc.vector.memset(scales[:].bitcast(I32), 0)
         for m in range(M // P):
-            nc.vector.memset(windows[m][:], 0.0)
+            nc.vector.memset(windows[m][:].bitcast(I32), 0)
 
         x_rows = xT.rearrange("(p j) w -> p j w", j=PACK)
 
@@ -64,10 +64,10 @@ def tile_list_hboth_bias_kernel(
                 source[0, 4 * q : 4 * q + 4, :].bitcast(I32),
             )
 
-        nc.sync.dma_start(lists_in[:], offs)
-        nc.sync.dma_start(wgt_t[0][:], wgt[:, 0:HALF])
+        nc.sync.dma_start(wgt_t[:, 0:HALF], wgt[:, 0:HALF])
         nc.sync.dma_start(planes[0][:], x_rows[:, 0, :])
-        nc.sync.dma_start(wgt_t[1][:], wgt[:, HALF:S])
+        nc.sync.dma_start(lists_in[:], offs)
+        nc.sync.dma_start(wgt_t[:, HALF:S], wgt[:, HALF:S])
         nc.sync.dma_start(planes[1][:], x_rows[:, 1, :])
         for q in range(3):
             load_scales(nc.sync, w4_scales, q, 0)
@@ -87,16 +87,16 @@ def tile_list_hboth_bias_kernel(
         def gather(t, c, lo=0, hi=HALF):
             first = c * HALF + lo
             nc.vector.tensor_tensor(
-                picked[c][:, t, lo:hi],
+                picked[t // 2][:, t % 2, first : first + hi - lo],
                 planes[t][:].indirect(lists_in[:, first // 16 : (first + hi - lo) // 16]),
-                wgt_t[c][:, lo:hi],
+                wgt_t[:, first : first + hi - lo],
                 MULT,
             )
 
         def group(copy, c, t0, lo=0, hi=HALF):
             copy(
                 grouped[c][:, lo:hi, t0 : t0 + 2],
-                picked[c][:, t0 : t0 + 2, lo:hi].rearrange("p t n -> p n t"),
+                picked[t0 // 2][:, :, c * HALF + lo : c * HALF + hi].rearrange("p t n -> p n t"),
             )
 
         def quantize(c, lo, hi):
@@ -143,8 +143,7 @@ def tile_list_hboth_bias_kernel(
             gather(t, 1)
         group(nc.scalar.copy, 0, 0)
         group(nc.scalar.copy, 1, 0)
-        gather(2, 0)
-        gather(2, 1)
+        gather(2, 0, 0, S)
         for h in range(2):
             gather(3, 0, h * N_MM, (h + 1) * N_MM)
         for h in range(2):

@@ -157,7 +157,8 @@ def tile_list_hboth_bias_kernel(
             gather(3, 1, h * N_MM, (h + 1) * N_MM)
         for h in range(2):
             group(nc.scalar.copy, 1, 2, h * N_MM, (h + 1) * N_MM)
-        quantize(1, 0, HALF)
+        for h in range(2):
+            quantize(1, h * N_MM, (h + 1) * N_MM)
         multiply(1, 1)
         multiply(1, 0)
         scatter(0, 0, 0, N_MM)

@@ -71,18 +71,18 @@ def tile_list_hboth_bias_kernel(
         nc.sync.dma_start(planes[1][:], x_rows[:, 1, :])
         for q in range(3):
             load_scales(nc.sync, w4_scales, q, 0)
-        for q in range(3):
-            load_scales(nc.gpsimd, r8_scales, q, M)
         nc.sync.dma_start(planes[2][:], x_rows[:, 2, :])
-        nc.sync.dma_start(planes[3][:], x_rows[:, 3, :])
         load_scales(nc.sync, w4_scales, 3, 0)
-        load_scales(nc.sync, r8_scales, 3, M)
+        load_scales(nc.sync, r8_scales, 0, M)
+        nc.sync.dma_start(planes[3][:], x_rows[:, 3, :])
+        for q in range(1, 4):
+            load_scales(nc.sync, r8_scales, q, M)
         nc.sync.dma_start(r8[:].bitcast(I32), r8_words[0].rearrange("p n i -> p (n i)").bitcast(I32))
         nc.sync.dma_start(w4[:].bitcast(I32), w4_words[0].bitcast(I32))
         nc.sync.dma_start(wgo_t[:], wgo)
-        nc.sync.dma_start(lists_out[:], offs2)
         with nc.allow_non_contiguous_dma(reason="one bias value to a partition"):
             nc.sync.dma_start(bias[:], b.rearrange("(m p) -> p m", p=P))
+        nc.sync.dma_start(lists_out[:], offs2)
 
         def gather(t, c, lo=0, hi=HALF):
             first = c * HALF + lo

@@ -42,15 +42,13 @@ def tile_list_hboth_bias_kernel(
         r8 = held.tile([P, 4 * M], U8, name="r8", align_bytes=64)
         scales = held.tile([P, 2 * M], U8, name="scales", align_bytes=64)
         windows = [held.tile([P, T], F32, name=f"window{m}") for m in range(M // P)]
-        picked = [held.tile([P, 2, S], F32, name=f"picked{pair}") for pair in range(2)]
-        grouped = [held.tile([P, HALF, PACK], BF16, name=f"grouped{c}", align_bytes=64) for c in range(2)]
-        codes = [held.tile([P, HALF], U32, name=f"codes{c}", align_bytes=64) for c in range(2)]
-        xscales = [held.tile([P, HALF], U8, name=f"xscales{c}", align_bytes=64) for c in range(2)]
-        y = [[held.tile([P, HALF], F32, name=f"y{c}{m}") for m in range(M // P)] for c in range(2)]
-        acc = [
-            [[psum.tile([P, N_MM], F32, name=f"acc{c}{m}{h}") for h in range(2)] for m in range(M // P)]
-            for c in range(2)
-        ]
+        picked01 = held.tile([P, 2, S], F32, name="picked01")
+        picked23 = held.tile([P, 2, S], F32, name="picked23")
+        grouped = held.tile([P, S, PACK], BF16, name="grouped", align_bytes=64)
+        codes = held.tile([P, S], U32, name="codes", align_bytes=64)
+        xscales = held.tile([P, S], U8, name="xscales", align_bytes=64)
+        y = [held.tile([P, S], F32, name=f"y{m}") for m in range(M // P)]
+        acc = [[psum.tile([P, N_MM], F32, name=f"acc{m}{i}") for i in range(S // N_MM)] for m in range(M // P)]
 
         nc.vector.memset(scales[:].bitcast(I32), 0)
         for m in range(M // P):
@@ -84,86 +82,66 @@ def tile_list_hboth_bias_kernel(
             nc.sync.dma_start(bias[:], b.rearrange("(m p) -> p m", p=P))
         nc.sync.dma_start(lists_out[:], offs2)
 
-        def gather(t, c, lo=0, hi=HALF):
-            first = c * HALF + lo
-            nc.vector.tensor_tensor(
-                picked[t // 2][:, t % 2, first : first + hi - lo],
-                planes[t][:].indirect(lists_in[:, first // 16 : (first + hi - lo) // 16]),
-                wgt_t[:, first : first + hi - lo],
-                MULT,
-            )
+        def gather(dst, t, lo, hi):
+            nc.vector.tensor_tensor(dst, planes[t][:].indirect(lists_in[:, lo // 16 : hi // 16]), wgt_t[:, lo:hi], MULT)
 
-        def group(copy, c, t0, lo=0, hi=HALF):
-            copy(
-                grouped[c][:, lo:hi, t0 : t0 + 2],
-                picked[t0 // 2][:, :, c * HALF + lo : c * HALF + hi].rearrange("p t n -> p n t"),
-            )
+        def group(pair, t0, lo, hi):
+            nc.scalar.copy(grouped[:, lo:hi, t0 : t0 + 2], pair.rearrange("p t n -> p n t"))
 
-        def quantize(c, lo, hi):
+        def quantize(lo, hi):
+            cols = slice(lo, hi)
             nc.vector.quantize_mx(
-                out=codes[c][:, lo:hi].bitcast(E4M3X4),
-                scales=xscales[c][:, lo:hi],
-                in_=grouped[c][:, lo:hi, :].rearrange("p n t -> p (n t)"),
+                out=codes[:, cols].bitcast(E4M3X4),
+                scales=xscales[:, cols],
+                in_=grouped[:, cols, :].rearrange("p n t -> p (n t)"),
             )
 
-        def multiply(c, m, halves=(0, 1)):
-            for h in halves:
-                cols = slice(h * N_MM, (h + 1) * N_MM)
-                nc.tensor.matmul_mx(
-                    out=acc[c][m][h][:],
-                    lhsT=w4[:, 2 * m * P : 2 * (m + 1) * P].bitcast(E2M1X4),
-                    lhsT_scale=scales[:, m * P : (m + 1) * P],
-                    rhs=codes[c][:, cols].bitcast(E4M3X4),
-                    rhs_scale=xscales[c][:, cols],
-                    start=True,
-                    stop=False,
-                )
-                nc.tensor.matmul_mx(
-                    out=acc[c][m][h][:],
-                    lhsT=r8[:, 4 * m * P : 4 * (m + 1) * P].bitcast(E4M3X4),
-                    lhsT_scale=scales[:, M + m * P : M + (m + 1) * P],
-                    rhs=codes[c][:, cols].bitcast(E4M3X4),
-                    rhs_scale=xscales[c][:, cols],
-                    start=False,
-                    stop=True,
-                )
-                nc.scalar.activation(y[c][m][:, cols], acc[c][m][h][:], IDENTITY, bias=bias[:, m : m + 1], scale=1.0)
+        def multiply(m, i):
+            cols = slice(i * N_MM, (i + 1) * N_MM)
+            nc.tensor.matmul_mx(
+                out=acc[m][i][:],
+                lhsT=w4[:, 2 * m * P : 2 * (m + 1) * P].bitcast(E2M1X4),
+                lhsT_scale=scales[:, m * P : (m + 1) * P],
+                rhs=codes[:, cols].bitcast(E4M3X4),
+                rhs_scale=xscales[:, cols],
+                start=True,
+                stop=False,
+            )
+            nc.tensor.matmul_mx(
+                out=acc[m][i][:],
+                lhsT=r8[:, 4 * m * P : 4 * (m + 1) * P].bitcast(E4M3X4),
+                lhsT_scale=scales[:, M + m * P : M + (m + 1) * P],
+                rhs=codes[:, cols].bitcast(E4M3X4),
+                rhs_scale=xscales[:, cols],
+                start=False,
+                stop=True,
+            )
+            nc.scalar.activation(y[m][:, cols], acc[m][i][:], IDENTITY, bias=bias[:, m : m + 1], scale=1.0)
 
-        def scatter(c, m, lo=0, hi=HALF):
-            first = c * HALF + lo
+        def scatter(m, lo, hi):
             nc.vector.tensor_tensor(
-                windows[m][:].indirect(lists_out[:, first // 16 : (first + hi - lo) // 16]),
-                y[c][m][:, lo:hi],
-                wgo_t[:, first : first + hi - lo],
-                MULT,
+                windows[m][:].indirect(lists_out[:, lo // 16 : hi // 16]), y[m][:, lo:hi], wgo_t[:, lo:hi], MULT
             )
 
         for t in range(2):
-            gather(t, 0)
-            gather(t, 1)
-        group(nc.scalar.copy, 0, 0)
-        group(nc.scalar.copy, 1, 0)
-        gather(2, 0, 0, S)
-        for h in range(2):
-            gather(3, 0, h * N_MM, (h + 1) * N_MM)
-        for h in range(2):
-            group(nc.scalar.copy, 0, 2, h * N_MM, (h + 1) * N_MM)
-        for h in range(2):
-            quantize(0, h * N_MM, (h + 1) * N_MM)
-        multiply(0, 0, (0,))
-        multiply(0, 1)
-        multiply(0, 0, (1,))
-        for h in range(2):
-            gather(3, 1, h * N_MM, (h + 1) * N_MM)
-        for h in range(2):
-            group(nc.scalar.copy, 1, 2, h * N_MM, (h + 1) * N_MM)
-        for h in range(2):
-            quantize(1, h * N_MM, (h + 1) * N_MM)
-        multiply(1, 1)
-        multiply(1, 0)
-        scatter(0, 0, 0, N_MM)
-        scatter(0, 1)
-        scatter(0, 0, N_MM, HALF)
-        for m in (1, 0):
-            scatter(1, m)
+            for lo in (0, HALF):
+                gather(picked01[:, t, lo : lo + HALF], t, lo, lo + HALF)
+        for lo in (0, HALF):
+            group(picked01[:, :, lo : lo + HALF], 0, lo, lo + HALF)
+        gather(picked23[:, 0, :], 2, 0, S)
+        for half in (0, HALF):
+            pieces = [(half, half + N_MM), (half + N_MM, half + HALF)]
+            for lo, hi in pieces:
+                gather(picked23[:, 1, lo:hi], 3, lo, hi)
+            for lo, hi in pieces:
+                group(picked23[:, :, lo:hi], 2, lo, hi)
+            for lo, hi in pieces:
+                quantize(lo, hi)
+            for m, i in ((0, 0), (1, 0), (0, 1), (1, 1)) if half == 0 else ((1, 2), (1, 3), (0, 2), (0, 3)):
+                multiply(m, i)
+        scatter(0, 0, N_MM)
+        scatter(1, 0, N_MM)
+        scatter(0, N_MM, HALF)
+        for m, lo in ((1, N_MM), (0, HALF)):
+            scatter(m, lo, S)
             nc.sync.dma_start(out[m * P : (m + 1) * P, :], windows[m][:])

@@ -66,14 +66,16 @@ def tile_list_hboth_bias_kernel(
         nc.sync.dma_start(planes[0][:], x_rows[:, 0, :])
         nc.sync.dma_start(lists_in[:], offs)
         nc.sync.dma_start(wgt_t[:, HALF:S], wgt[:, HALF:S])
+        load_scales(nc.sync, w4_scales, 0, 0)
         nc.sync.dma_start(planes[1][:], x_rows[:, 1, :])
-        for q in range(3):
+        for q in range(1, 3):
             load_scales(nc.sync, w4_scales, q, 0)
         nc.sync.dma_start(planes[2][:], x_rows[:, 2, :])
         load_scales(nc.sync, w4_scales, 3, 0)
-        load_scales(nc.sync, r8_scales, 0, M)
+        for q in range(2):
+            load_scales(nc.sync, r8_scales, q, M)
         nc.sync.dma_start(planes[3][:], x_rows[:, 3, :])
-        for q in range(1, 4):
+        for q in range(2, 4):
             load_scales(nc.sync, r8_scales, q, M)
         nc.sync.dma_start(r8[:].bitcast(I32), r8_words[0].rearrange("p n i -> p (n i)").bitcast(I32))
         nc.sync.dma_start(w4[:].bitcast(I32), w4_words[0].bitcast(I32))

@@ -146,4 +146,4 @@ def tile_list_hboth_bias_kernel(
         scatter(0, N_MM, HALF)
         for m, lo in ((1, N_MM), (0, HALF)):
             scatter(m, lo, S)
-            nc.sync.dma_start(out[m * P : (m + 1) * P, :], windows[m][:])
+            nc.scalar.dma_start(out[m * P : (m + 1) * P, :], windows[m][:])

@@ -34,7 +34,9 @@ def tile_list_hboth_bias_kernel(
 
         lists_in = held.tile([P, S // 16], U16, name="lists_in")
         lists_out = held.tile([P, S // 16], U16, name="lists_out")
-        wgt_t = held.tile([P, S], F32, name="wgt_t")
+        places = held.tile([P, 10, N_MM], F32, name="places")
+        flat = places[:].rearrange("p i n -> p (i n)")
+        wgt_t = flat[:, 0:S]
         wgo_t = held.tile([P, S], F32, name="wgo_t")
         bias = held.tile([P, M // P], F32, name="bias")
         planes = [held.tile([P, T], F32, name=f"plane{t}") for t in range(PACK)]
@@ -43,7 +45,6 @@ def tile_list_hboth_bias_kernel(
         scales = held.tile([P, 2 * M], U8, name="scales", align_bytes=64)
         windows = [held.tile([P, T], F32, name=f"window{m}") for m in range(M // P)]
         picked01 = held.tile([P, 2, S], F32, name="picked01")
-        picked23 = held.tile([P, 2, S], F32, name="picked23")
         grouped = held.tile([P, S, PACK], BF16, name="grouped", align_bytes=64)
         codes = held.tile([P, S], U32, name="codes", align_bytes=64)
         xscales = held.tile([P, S], U8, name="xscales", align_bytes=64)
@@ -130,17 +131,22 @@ def tile_list_hboth_bias_kernel(
                 gather(picked01[:, t, lo : lo + HALF], t, lo, lo + HALF)
         for lo in (0, HALF):
             group(picked01[:, :, lo : lo + HALF], 0, lo, lo + HALF)
-        gather(picked23[:, 0, :], 2, 0, S)
-        for half in (0, HALF):
-            pieces = [(half, half + N_MM), (half + N_MM, half + HALF)]
-            for lo, hi in pieces:
-                gather(picked23[:, 1, lo:hi], 3, lo, hi)
-            for lo, hi in pieces:
-                group(picked23[:, :, lo:hi], 2, lo, hi)
-            for lo, hi in pieces:
-                quantize(lo, hi)
-            for m, i in ((0, 0), (1, 0), (0, 1), (1, 1)) if half == 0 else ((1, 2), (1, 3), (0, 2), (0, 3)):
-                multiply(m, i)
+        gather(flat[:, S : S + 3 * N_MM], 2, 0, 3 * N_MM)
+        for i in range(3):
+            gather(places[:, 7 + i, :], 3, i * N_MM, (i + 1) * N_MM)
+        gather(places[:, 0, :], 2, 3 * N_MM, S)
+
+        def finish(i, pair):
+            group(pair, 2, i * N_MM, (i + 1) * N_MM)
+            quantize(i * N_MM, (i + 1) * N_MM)
+
+        finish(0, places[:, 4:8:3, :])
+        gather(places[:, 4, :], 3, 3 * N_MM, S)
+        finish(1, places[:, 5:9:3, :])
+        finish(2, places[:, 6:10:3, :])
+        finish(3, places[:, 0:5:4, :])
+        for m, i in ((0, 0), (1, 0), (0, 1), (1, 1), (1, 2), (1, 3), (0, 2), (0, 3)):
+            multiply(m, i)
         scatter(0, 0, N_MM)
         scatter(1, 0, N_MM)
         scatter(0, N_MM, HALF)

@@ -63,10 +63,9 @@ def tile_list_hboth_bias_kernel(
                 source[0, 4 * q : 4 * q + 4, :].bitcast(I32),
             )
 
-        nc.sync.dma_start(wgt_t[:, 0:HALF], wgt[:, 0:HALF])
+        nc.sync.dma_start(wgt_t, wgt)
         nc.sync.dma_start(planes[0][:], x_rows[:, 0, :])
         nc.sync.dma_start(lists_in[:], offs)
-        nc.sync.dma_start(wgt_t[:, HALF:S], wgt[:, HALF:S])
         load_scales(nc.sync, w4_scales, 0, 0)
         nc.sync.dma_start(planes[1][:], x_rows[:, 1, :])
         for q in range(1, 3):
@@ -126,9 +125,9 @@ def tile_list_hboth_bias_kernel(
                 windows[m][:].indirect(lists_out[:, lo // 16 : hi // 16]), y[m][:, lo:hi], wgo_t[:, lo:hi], MULT
             )
 
-        for t in range(2):
-            for lo in (0, HALF):
-                gather(picked01[:, t, lo : lo + HALF], t, lo, lo + HALF)
+        gather(picked01[:, 0, :], 0, 0, S)
+        for lo in (0, HALF):
+            gather(picked01[:, 1, lo : lo + HALF], 1, lo, lo + HALF)
         for lo in (0, HALF):
             group(picked01[:, :, lo : lo + HALF], 0, lo, lo + HALF)
         gather(flat[:, S : S + 3 * N_MM], 2, 0, 3 * N_MM)

@@ -21,6 +21,8 @@ PACK = 4
 HALF = S // 2
 LIST_COLS = HALF // 16
 N_MM = 128
+BLOCK = 32
+GROUP = 16
 FLOPS = 2 * 2 * K * M * S
 
 
@@ -34,9 +36,11 @@ def tile_list_hboth_bias_kernel(
 
         lists_in = held.tile([P, S // 16], U16, name="lists_in")
         lists_out = held.tile([P, S // 16], U16, name="lists_out")
-        places = held.tile([P, 10, N_MM], F32, name="places")
-        flat = places[:].rearrange("p i n -> p (i n)")
-        wgt_t = flat[:, 0:S]
+        picks = held.tile([P, PACK * S], F32, name="picks")
+        wgt_t = held.tile([P, S], F32, name="wgt_t", align_bytes=64)
+        wgt_runs = held.tile([P, BLOCK], F32, name="wgt_runs", align_bytes=64)
+        wgt_turned = held.tile([P, BLOCK], F32, name="wgt_turned", align_bytes=64)
+        wgt_wide = held.tile([P, S], F32, name="wgt_wide", align_bytes=64)
         wgo_t = held.tile([P, S], F32, name="wgo_t")
         bias = held.tile([P, M // P], F32, name="bias")
         planes = [held.tile([P, T], F32, name=f"plane{t}") for t in range(PACK)]
@@ -44,16 +48,17 @@ def tile_list_hboth_bias_kernel(
         r8 = held.tile([P, 4 * M], U8, name="r8", align_bytes=64)
         scales = held.tile([P, 2 * M], U8, name="scales", align_bytes=64)
         windows = [held.tile([P, T], F32, name=f"window{m}") for m in range(M // P)]
-        picked01 = held.tile([P, 2, S], F32, name="picked01")
-        grouped = held.tile([P, S, PACK], BF16, name="grouped", align_bytes=64)
-        codes = held.tile([P, S], U32, name="codes", align_bytes=64)
+        grouped = held.tile([P, HALF, PACK], BF16, name="grouped", align_bytes=64)
+        codes0 = held.tile([P, N_MM], U32, name="codes0", tag="first_codes", align_bytes=64)
+        codes = held.tile([P, S - N_MM], U32, name="codes", align_bytes=64)
         xscales = held.tile([P, S], U8, name="xscales", align_bytes=64)
         y = [held.tile([P, S], F32, name=f"y{m}") for m in range(M // P)]
-        acc = [[psum.tile([P, N_MM], F32, name=f"acc{m}{i}") for i in range(S // N_MM)] for m in range(M // P)]
+        widths = (N_MM, N_MM, HALF)
+        acc = [[psum.tile([P, w], F32, name=f"acc{m}{i}") for i, w in enumerate(widths)] for m in range(M // P)]
 
         nc.vector.memset(scales[:].bitcast(I32), 0)
-        for m in range(M // P):
-            nc.vector.memset(windows[m][:].bitcast(I32), 0)
+        nc.vector.memset(windows[0][:].bitcast(I32), 0)
+        nc.gpsimd.memset(windows[1][:].bitcast(I32), 0)
 
         x_rows = xT.rearrange("(p j) w -> p j w", j=PACK)
 
@@ -63,7 +68,7 @@ def tile_list_hboth_bias_kernel(
                 source[0, 4 * q : 4 * q + 4, :].bitcast(I32),
             )
 
-        nc.sync.dma_start(wgt_t, wgt)
+        nc.sync.dma_start(wgt_runs[:], wgt.rearrange("(g r) j -> g r j", r=GROUP)[:, 0, :])
         nc.sync.dma_start(planes[0][:], x_rows[:, 0, :])
         nc.sync.dma_start(lists_in[:], offs)
         load_scales(nc.sync, w4_scales, 0, 0)
@@ -75,80 +80,100 @@ def tile_list_hboth_bias_kernel(
         for q in range(2):
             load_scales(nc.sync, r8_scales, q, M)
         nc.sync.dma_start(planes[3][:], x_rows[:, 3, :])
+        nc.sync.dma_start(wgo_t[:], wgo)
+        nc.sync.dma_start(r8[:].bitcast(I32), r8_words[0].rearrange("p n i -> p (n i)").bitcast(I32))
         for q in range(2, 4):
             load_scales(nc.sync, r8_scales, q, M)
-        nc.sync.dma_start(r8[:].bitcast(I32), r8_words[0].rearrange("p n i -> p (n i)").bitcast(I32))
-        nc.sync.dma_start(w4[:].bitcast(I32), w4_words[0].bitcast(I32))
-        nc.sync.dma_start(wgo_t[:], wgo)
+        nc.sync.dma_start(lists_out[:], offs2)
         with nc.allow_non_contiguous_dma(reason="one bias value to a partition"):
             nc.sync.dma_start(bias[:], b.rearrange("(m p) -> p m", p=P))
-        nc.sync.dma_start(lists_out[:], offs2)
+        nc.sync.dma_start(w4[:].bitcast(I32), w4_words[0].bitcast(I32))
 
-        def gather(dst, t, lo, hi):
-            nc.vector.tensor_tensor(dst, planes[t][:].indirect(lists_in[:, lo // 16 : hi // 16]), wgt_t[:, lo:hi], MULT)
+        nc.vector.transpose(wgt_turned[:], wgt_runs[:])
+        turned = wgt_turned[:].rearrange("p (h k) -> p k h", h=2)
+        for lo in (0, HALF):
+            nc.vector.tensor_copy(
+                wgt_wide[:, lo : lo + HALF].rearrange("p (k h r) -> p k h r", h=2, r=GROUP),
+                turned[:, lo // BLOCK : (lo + HALF) // BLOCK, :].unsqueeze(3).to_broadcast([P, HALF // BLOCK, 2, GROUP]),
+            )
+        for lo in (0, HALF):
+            nc.vector.transpose(wgt_t[:, lo : lo + HALF], wgt_wide[:, lo : lo + HALF])
 
-        def group(pair, t0, lo, hi):
-            nc.scalar.copy(grouped[:, lo:hi, t0 : t0 + 2], pair.rearrange("p t n -> p n t"))
-
-        def quantize(lo, hi):
-            cols = slice(lo, hi)
-            nc.vector.quantize_mx(
-                out=codes[:, cols].bitcast(E4M3X4),
-                scales=xscales[:, cols],
-                in_=grouped[:, cols, :].rearrange("p n t -> p (n t)"),
+        def gather(place, t, lo, hi):
+            nc.vector.tensor_tensor(
+                picks[:, place * N_MM : place * N_MM + hi - lo],
+                planes[t][:].indirect(lists_in[:, lo // 16 : hi // 16]),
+                wgt_t[:, lo:hi],
+                MULT,
             )
 
-        def multiply(m, i):
-            cols = slice(i * N_MM, (i + 1) * N_MM)
+        places = picks[:].rearrange("p (i n) -> p i n", n=N_MM)
+        by_plane = picks[:].rearrange("p (t n) -> p n t", t=PACK)
+
+        def quantize(dst, lo, hi, src):
+            nc.vector.quantize_mx(
+                out=dst.bitcast(E4M3X4), scales=xscales[:, lo:hi], in_=src.rearrange("p n t -> p (n t)")
+            )
+
+        def multiply(dst, m, rhs, lo):
             nc.tensor.matmul_mx(
-                out=acc[m][i][:],
+                out=dst,
                 lhsT=w4[:, 2 * m * P : 2 * (m + 1) * P].bitcast(E2M1X4),
                 lhsT_scale=scales[:, m * P : (m + 1) * P],
-                rhs=codes[:, cols].bitcast(E4M3X4),
-                rhs_scale=xscales[:, cols],
+                rhs=rhs.bitcast(E4M3X4),
+                rhs_scale=xscales[:, lo : lo + N_MM],
                 start=True,
                 stop=False,
             )
             nc.tensor.matmul_mx(
-                out=acc[m][i][:],
+                out=dst,
                 lhsT=r8[:, 4 * m * P : 4 * (m + 1) * P].bitcast(E4M3X4),
                 lhsT_scale=scales[:, M + m * P : M + (m + 1) * P],
-                rhs=codes[:, cols].bitcast(E4M3X4),
-                rhs_scale=xscales[:, cols],
+                rhs=rhs.bitcast(E4M3X4),
+                rhs_scale=xscales[:, lo : lo + N_MM],
                 start=False,
                 stop=True,
             )
-            nc.scalar.activation(y[m][:, cols], acc[m][i][:], IDENTITY, bias=bias[:, m : m + 1], scale=1.0)
+
+        def add_bias(m, i, lo, hi):
+            nc.scalar.activation(y[m][:, lo:hi], acc[m][i][:], IDENTITY, bias=bias[:, m : m + 1], scale=1.0)
 
         def scatter(m, lo, hi):
             nc.vector.tensor_tensor(
                 windows[m][:].indirect(lists_out[:, lo // 16 : hi // 16]), y[m][:, lo:hi], wgo_t[:, lo:hi], MULT
             )
 
-        gather(picked01[:, 0, :], 0, 0, S)
         for lo in (0, HALF):
-            gather(picked01[:, 1, lo : lo + HALF], 1, lo, lo + HALF)
-        for lo in (0, HALF):
-            group(picked01[:, :, lo : lo + HALF], 0, lo, lo + HALF)
-        gather(flat[:, S : S + 3 * N_MM], 2, 0, 3 * N_MM)
-        for i in range(3):
-            gather(places[:, 7 + i, :], 3, i * N_MM, (i + 1) * N_MM)
-        gather(places[:, 0, :], 2, 3 * N_MM, S)
-
-        def finish(i, pair):
-            group(pair, 2, i * N_MM, (i + 1) * N_MM)
-            quantize(i * N_MM, (i + 1) * N_MM)
-
-        finish(0, places[:, 4:8:3, :])
-        gather(places[:, 4, :], 3, 3 * N_MM, S)
-        finish(1, places[:, 5:9:3, :])
-        finish(2, places[:, 6:10:3, :])
-        finish(3, places[:, 0:5:4, :])
-        for m, i in ((0, 0), (1, 0), (0, 1), (1, 1), (1, 2), (1, 3), (0, 2), (0, 3)):
-            multiply(m, i)
-        scatter(0, 0, N_MM)
-        scatter(1, 0, N_MM)
-        scatter(0, N_MM, HALF)
-        for m, lo in ((1, N_MM), (0, HALF)):
-            scatter(m, lo, S)
+            gather(lo // N_MM, 0, lo, lo + HALF)
+        gather(4, 1, 0, S)
+        nc.scalar.copy(grouped[:, :, 0:2], by_plane[:, 0:HALF, 0:2])
+        gather(11, 2, 0, HALF)
+        gather(15, 3, 0, N_MM)
+        gather(13, 3, N_MM, 3 * N_MM)
+        nc.scalar.copy(grouped[:, 0:N_MM, 2:4], places[:, 11:16:4, :].rearrange("p t n -> p n t"))
+        quantize(codes0[:], 0, N_MM, grouped[:, 0:N_MM, :])
+        nc.scalar.copy(grouped[:, N_MM:HALF, 2:4], places[:, 12:14, :].rearrange("p t n -> p n t"))
+        gather(10, 2, HALF, S)
+        gather(15, 3, 3 * N_MM, S)
+        quantize(codes[:, 0:N_MM], N_MM, HALF, grouped[:, N_MM:HALF, :])
+        for m in range(M // P):
+            multiply(acc[m][0][:], m, codes0[:], 0)
+            add_bias(m, 0, 0, N_MM)
+        for m in range(M // P):
+            scatter(m, 0, N_MM)
+        grouped_late = held.tile([P, HALF, PACK], BF16, name="grouped_late", tag="first_codes", align_bytes=64)
+        nc.scalar.copy(grouped_late[:], by_plane[:, HALF:S, :])
+        quantize(codes[:, N_MM:], HALF, S, grouped_late[:])
+        for m in range(M // P):
+            multiply(acc[m][1][:], m, codes[:, 0:N_MM], N_MM)
+            add_bias(m, 1, N_MM, HALF)
+        for m in range(M // P):
+            scatter(m, N_MM, HALF)
+        for m in range(M // P):
+            for i in range(2):
+                lo = HALF + i * N_MM
+                multiply(acc[m][2][:, i * N_MM : (i + 1) * N_MM], m, codes[:, lo - N_MM : lo], lo)
+            add_bias(m, 2, HALF, S)
+        for m in range(M // P):
+            scatter(m, HALF, S)
             nc.scalar.dma_start(out[m * P : (m + 1) * P, :], windows[m][:])

@@ -36,7 +36,7 @@ def tile_list_hboth_bias_kernel(
 
         lists_in = held.tile([P, S // 16], U16, name="lists_in")
         lists_out = held.tile([P, S // 16], U16, name="lists_out")
-        picks = held.tile([P, PACK * S], F32, name="picks")
+        picks = held.tile([P, 18 * N_MM], F32, name="picks")
         wgt_t = held.tile([P, S], F32, name="wgt_t", align_bytes=64)
         wgt_runs = held.tile([P, BLOCK], F32, name="wgt_runs", align_bytes=64)
         wgt_turned = held.tile([P, BLOCK], F32, name="wgt_turned", align_bytes=64)
@@ -48,13 +48,13 @@ def tile_list_hboth_bias_kernel(
         r8 = held.tile([P, 4 * M], U8, name="r8", align_bytes=64)
         scales = held.tile([P, 2 * M], U8, name="scales", align_bytes=64)
         windows = [held.tile([P, T], F32, name=f"window{m}") for m in range(M // P)]
-        grouped = held.tile([P, HALF, PACK], BF16, name="grouped", align_bytes=64)
+        grouped = held.tile([P, 3 * N_MM, PACK], BF16, name="grouped", align_bytes=64)
         codes0 = held.tile([P, N_MM], U32, name="codes0", tag="first_codes", align_bytes=64)
-        codes = held.tile([P, S - N_MM], U32, name="codes", align_bytes=64)
+        codes1 = held.tile([P, HALF], U32, name="codes1", align_bytes=64)
+        y_first = held.tile([P, N_MM], F32, name="y_first", tag="first_y", align_bytes=64)
         xscales = held.tile([P, S], U8, name="xscales", align_bytes=64)
         y = [held.tile([P, S], F32, name=f"y{m}") for m in range(M // P)]
-        widths = (N_MM, N_MM, HALF)
-        acc = [[psum.tile([P, w], F32, name=f"acc{m}{i}") for i, w in enumerate(widths)] for m in range(M // P)]
+        acc = [[psum.tile([P, N_MM], F32, name=f"acc{m}{i}") for i in range(S // N_MM)] for m in range(M // P)]
 
         nc.vector.memset(scales[:].bitcast(I32), 0)
         nc.vector.memset(windows[0][:].bitcast(I32), 0)
@@ -71,23 +71,22 @@ def tile_list_hboth_bias_kernel(
         nc.sync.dma_start(wgt_runs[:], wgt.rearrange("(g r) j -> g r j", r=GROUP)[:, 0, :])
         nc.sync.dma_start(planes[0][:], x_rows[:, 0, :])
         nc.sync.dma_start(lists_in[:], offs)
-        load_scales(nc.sync, w4_scales, 0, 0)
-        nc.sync.dma_start(planes[1][:], x_rows[:, 1, :])
-        for q in range(1, 3):
+        for q in range(3):
             load_scales(nc.sync, w4_scales, q, 0)
-        nc.sync.dma_start(planes[2][:], x_rows[:, 2, :])
+        nc.sync.dma_start(planes[1][:], x_rows[:, 1, :])
         load_scales(nc.sync, w4_scales, 3, 0)
+        nc.sync.dma_start(planes[2][:], x_rows[:, 2, :])
         for q in range(2):
             load_scales(nc.sync, r8_scales, q, M)
         nc.sync.dma_start(planes[3][:], x_rows[:, 3, :])
-        nc.sync.dma_start(wgo_t[:], wgo)
         nc.sync.dma_start(r8[:].bitcast(I32), r8_words[0].rearrange("p n i -> p (n i)").bitcast(I32))
-        for q in range(2, 4):
-            load_scales(nc.sync, r8_scales, q, M)
-        nc.sync.dma_start(lists_out[:], offs2)
         with nc.allow_non_contiguous_dma(reason="one bias value to a partition"):
             nc.sync.dma_start(bias[:], b.rearrange("(m p) -> p m", p=P))
+        for q in range(2, 4):
+            load_scales(nc.sync, r8_scales, q, M)
         nc.sync.dma_start(w4[:].bitcast(I32), w4_words[0].bitcast(I32))
+        nc.sync.dma_start(wgo_t[:], wgo)
+        nc.sync.dma_start(lists_out[:], offs2)
 
         nc.vector.transpose(wgt_turned[:], wgt_runs[:])
         turned = wgt_turned[:].rearrange("p (h k) -> p k h", h=2)
@@ -108,7 +107,7 @@ def tile_list_hboth_bias_kernel(
             )
 
         places = picks[:].rearrange("p (i n) -> p i n", n=N_MM)
-        by_plane = picks[:].rearrange("p (t n) -> p n t", t=PACK)
+        by_plane = picks[:, 0 : PACK * S].rearrange("p (t n) -> p n t", t=PACK)
 
         def quantize(dst, lo, hi, src):
             nc.vector.quantize_mx(
@@ -135,45 +134,54 @@ def tile_list_hboth_bias_kernel(
                 stop=True,
             )
 
+        def sums(m, lo, hi):
+            return y_first[:] if (m, lo) == (1, 0) else y[m][:, lo:hi]
+
         def add_bias(m, i, lo, hi):
-            nc.scalar.activation(y[m][:, lo:hi], acc[m][i][:], IDENTITY, bias=bias[:, m : m + 1], scale=1.0)
+            nc.scalar.activation(sums(m, lo, hi), acc[m][i][:], IDENTITY, bias=bias[:, m : m + 1], scale=1.0)
 
         def scatter(m, lo, hi):
             nc.vector.tensor_tensor(
-                windows[m][:].indirect(lists_out[:, lo // 16 : hi // 16]), y[m][:, lo:hi], wgo_t[:, lo:hi], MULT
+                windows[m][:].indirect(lists_out[:, lo // 16 : hi // 16]), sums(m, lo, hi), wgo_t[:, lo:hi], MULT
             )
 
         for lo in (0, HALF):
             gather(lo // N_MM, 0, lo, lo + HALF)
-        gather(4, 1, 0, S)
-        nc.scalar.copy(grouped[:, :, 0:2], by_plane[:, 0:HALF, 0:2])
-        gather(11, 2, 0, HALF)
+        for lo in (0, HALF):
+            gather(4 + lo // N_MM, 1, lo, lo + HALF)
+        last = 3 * N_MM
+        for lo, hi in ((0, HALF), (HALF, last)):
+            nc.scalar.copy(grouped[:, lo:hi, 0:2], by_plane[:, lo:hi, 0:2])
+        gather(11, 2, 0, last)
         gather(15, 3, 0, N_MM)
-        gather(13, 3, N_MM, 3 * N_MM)
+        gather(16, 3, N_MM, last)
         nc.scalar.copy(grouped[:, 0:N_MM, 2:4], places[:, 11:16:4, :].rearrange("p t n -> p n t"))
         quantize(codes0[:], 0, N_MM, grouped[:, 0:N_MM, :])
-        nc.scalar.copy(grouped[:, N_MM:HALF, 2:4], places[:, 12:14, :].rearrange("p t n -> p n t"))
-        gather(10, 2, HALF, S)
-        gather(15, 3, 3 * N_MM, S)
-        quantize(codes[:, 0:N_MM], N_MM, HALF, grouped[:, N_MM:HALF, :])
-        for m in range(M // P):
-            multiply(acc[m][0][:], m, codes0[:], 0)
-            add_bias(m, 0, 0, N_MM)
-        for m in range(M // P):
+        middle = picks[:, 10 * N_MM :].rearrange("p (t n) -> p n t", t=2)
+        nc.scalar.copy(grouped[:, N_MM:last, 2:4], middle[:, HALF:S, :])
+        gather(11, 2, last, S)
+        gather(15, 3, last, S)
+        quantize(codes1[:], N_MM, last, grouped[:, N_MM:last, :])
+
+        def product(m, i, rhs):
+            multiply(acc[m][i][:], m, rhs, i * N_MM)
+            add_bias(m, i, i * N_MM, (i + 1) * N_MM)
+
+        for m in (1, 0):
+            product(m, 0, codes0[:])
+        for m in (1, 0):
             scatter(m, 0, N_MM)
-        grouped_late = held.tile([P, HALF, PACK], BF16, name="grouped_late", tag="first_codes", align_bytes=64)
-        nc.scalar.copy(grouped_late[:], by_plane[:, HALF:S, :])
-        quantize(codes[:, N_MM:], HALF, S, grouped_late[:])
-        for m in range(M // P):
-            multiply(acc[m][1][:], m, codes[:, 0:N_MM], N_MM)
-            add_bias(m, 1, N_MM, HALF)
-        for m in range(M // P):
-            scatter(m, N_MM, HALF)
-        for m in range(M // P):
-            for i in range(2):
-                lo = HALF + i * N_MM
-                multiply(acc[m][2][:, i * N_MM : (i + 1) * N_MM], m, codes[:, lo - N_MM : lo], lo)
-            add_bias(m, 2, HALF, S)
-        for m in range(M // P):
-            scatter(m, HALF, S)
+        grouped_late = held.tile([P, N_MM, PACK], BF16, name="grouped_late", tag="first_codes", align_bytes=64)
+        nc.scalar.copy(grouped_late[:], by_plane[:, last:S, :])
+        codes_late = held.tile([P, N_MM], U32, name="codes_late", tag="first_y", align_bytes=64)
+        quantize(codes_late[:], last, S, grouped_late[:])
+        for m in (1, 0):
+            for i in (1, 2):
+                product(m, i, codes1[:, (i - 1) * N_MM : i * N_MM])
+        scatter(1, N_MM, last)
+        scatter(0, N_MM, HALF)
+        for m in (1, 0):
+            product(m, 3, codes_late[:])
+        for m, lo in ((1, last), (0, HALF)):
+            scatter(m, lo, S)
             nc.scalar.dma_start(out[m * P : (m + 1) * P, :], windows[m][:])

@@ -1,6 +1,7 @@
 from contextlib import ExitStack
 
 import concourse.mybir as mybir
+from concourse.masks import make_identity
 
 K, M, T, S = 512, 256, 1024, 512
 
@@ -43,6 +44,8 @@ def tile_list_hboth_bias_kernel(
         wgt_wide = held.tile([P, S], F32, name="wgt_wide", align_bytes=64)
         wgo_t = held.tile([P, S], F32, name="wgo_t")
         bias = held.tile([P, M // P], F32, name="bias")
+        bias_rows = held.tile([P, P], F32, name="bias_rows", align_bytes=64)
+        identity = held.tile([P, P], F32, name="identity", align_bytes=64)
         planes = [held.tile([P, T], F32, name=f"plane{t}") for t in range(PACK)]
         w4 = held.tile([P, 2 * M], U8, name="w4", align_bytes=64)
         r8 = held.tile([P, 4 * M], U8, name="r8", align_bytes=64)
@@ -54,11 +57,13 @@ def tile_list_hboth_bias_kernel(
         y_first = held.tile([P, N_MM], F32, name="y_first", tag="first_y", align_bytes=64)
         xscales = held.tile([P, S], U8, name="xscales", align_bytes=64)
         y = [held.tile([P, S], F32, name=f"y{m}") for m in range(M // P)]
-        acc = [[psum.tile([P, N_MM], F32, name=f"acc{m}{i}") for i in range(S // N_MM)] for m in range(M // P)]
+        bias_turned = psum.tile([P, P], F32, name="bias_turned", tag="acc03")
 
+        nc.vector.memset(bias_rows[:], 0.0)
         nc.vector.memset(scales[:].bitcast(I32), 0)
-        nc.vector.memset(windows[0][:].bitcast(I32), 0)
-        nc.gpsimd.memset(windows[1][:].bitcast(I32), 0)
+        make_identity(nc, identity[:])
+        for m in range(M // P):
+            nc.vector.memset(windows[m][:].bitcast(I32), 0)
 
         x_rows = xT.rearrange("(p j) w -> p j w", j=PACK)
 
@@ -71,7 +76,8 @@ def tile_list_hboth_bias_kernel(
         nc.sync.dma_start(wgt_runs[:], wgt.rearrange("(g r) j -> g r j", r=GROUP)[:, 0, :])
         nc.sync.dma_start(planes[0][:], x_rows[:, 0, :])
         nc.sync.dma_start(lists_in[:], offs)
-        for q in range(3):
+        nc.sync.dma_start(bias_rows[0 : M // P, :], b.rearrange("(m p) -> m p", p=P))
+        for q in range(2):
             load_scales(nc.sync, w4_scales, q, 0)
         nc.sync.dma_start(planes[1][:], x_rows[:, 1, :])
         load_scales(nc.sync, w4_scales, 3, 0)
@@ -80,8 +86,7 @@ def tile_list_hboth_bias_kernel(
             load_scales(nc.sync, r8_scales, q, M)
         nc.sync.dma_start(planes[3][:], x_rows[:, 3, :])
         nc.sync.dma_start(r8[:].bitcast(I32), r8_words[0].rearrange("p n i -> p (n i)").bitcast(I32))
-        with nc.allow_non_contiguous_dma(reason="one bias value to a partition"):
-            nc.sync.dma_start(bias[:], b.rearrange("(m p) -> p m", p=P))
+        load_scales(nc.sync, w4_scales, 2, 0)
         for q in range(2, 4):
             load_scales(nc.sync, r8_scales, q, M)
         nc.sync.dma_start(w4[:].bitcast(I32), w4_words[0].bitcast(I32))
@@ -97,6 +102,10 @@ def tile_list_hboth_bias_kernel(
             )
         for lo in (0, HALF):
             nc.vector.transpose(wgt_t[:, lo : lo + HALF], wgt_wide[:, lo : lo + HALF])
+
+        nc.tensor.transpose(bias_turned[:], bias_rows[:], identity[:])
+        nc.scalar.copy(bias[:], bias_turned[:, 0 : M // P])
+        acc = [[psum.tile([P, N_MM], F32, name=f"acc{m}{i}", tag=f"acc{m}{i}") for i in range(S // N_MM)] for m in range(M // P)]
 
         def gather(place, t, lo, hi):
             nc.vector.tensor_tensor(

@@ -82,12 +82,10 @@ def tile_list_hboth_bias_kernel(
         nc.sync.dma_start(planes[1][:], x_rows[:, 1, :])
         load_scales(nc.sync, w4_scales, 3, 0)
         nc.sync.dma_start(planes[2][:], x_rows[:, 2, :])
-        for q in range(2):
-            load_scales(nc.sync, r8_scales, q, M)
         nc.sync.dma_start(planes[3][:], x_rows[:, 3, :])
         nc.sync.dma_start(r8[:].bitcast(I32), r8_words[0].rearrange("p n i -> p (n i)").bitcast(I32))
         load_scales(nc.sync, w4_scales, 2, 0)
-        for q in range(2, 4):
+        for q in range(4):
             load_scales(nc.sync, r8_scales, q, M)
         nc.sync.dma_start(w4[:].bitcast(I32), w4_words[0].bitcast(I32))
         nc.sync.dma_start(wgo_t[:], wgo)

@@ -154,10 +154,9 @@ def tile_list_hboth_bias_kernel(
 
         for lo in (0, HALF):
             gather(lo // N_MM, 0, lo, lo + HALF)
-        for lo in (0, HALF):
-            gather(4 + lo // N_MM, 1, lo, lo + HALF)
+        gather(4, 1, 0, S)
         last = 3 * N_MM
-        for lo, hi in ((0, HALF), (HALF, last)):
+        for lo, hi in ((0, N_MM), (N_MM, last)):
             nc.scalar.copy(grouped[:, lo:hi, 0:2], by_plane[:, lo:hi, 0:2])
         gather(11, 2, 0, last)
         gather(15, 3, 0, N_MM)

@@ -41,7 +41,7 @@ def tile_list_hboth_bias_kernel(
         wgt_t = held.tile([P, S], F32, name="wgt_t", align_bytes=64)
         wgt_runs = held.tile([P, BLOCK], F32, name="wgt_runs", align_bytes=64)
         wgt_turned = held.tile([P, BLOCK], F32, name="wgt_turned", align_bytes=64)
-        wgt_wide = held.tile([P, S], F32, name="wgt_wide", align_bytes=64)
+        wgt_wide = held.tile([P, S], F32, name="wgt_wide", tag="wide_then_window", align_bytes=64)
         wgo_t = held.tile([P, S], F32, name="wgo_t")
         bias = held.tile([P, M // P], F32, name="bias")
         bias_rows = held.tile([P, P], F32, name="bias_rows", align_bytes=64)
@@ -50,7 +50,7 @@ def tile_list_hboth_bias_kernel(
         w4 = held.tile([P, 2 * M], U8, name="w4", align_bytes=64)
         r8 = held.tile([P, 4 * M], U8, name="r8", align_bytes=64)
         scales = held.tile([P, 2 * M], U8, name="scales", align_bytes=64)
-        windows = [held.tile([P, T], F32, name=f"window{m}") for m in range(M // P)]
+        window1 = held.tile([P, T], F32, name="window1")
         grouped = held.tile([P, 3 * N_MM, PACK], BF16, name="grouped", align_bytes=64)
         codes0 = held.tile([P, N_MM], U32, name="codes0", tag="first_codes", align_bytes=64)
         codes1 = held.tile([P, HALF], U32, name="codes1", align_bytes=64)
@@ -62,8 +62,7 @@ def tile_list_hboth_bias_kernel(
         nc.vector.memset(bias_rows[:], 0.0)
         nc.vector.memset(scales[:].bitcast(I32), 0)
         make_identity(nc, identity[:])
-        for m in range(M // P):
-            nc.vector.memset(windows[m][:].bitcast(I32), 0)
+        nc.vector.memset(window1[:].bitcast(I32), 0)
 
         x_rows = xT.rearrange("(p j) w -> p j w", j=PACK)
 
@@ -100,6 +99,10 @@ def tile_list_hboth_bias_kernel(
             )
         for lo in (0, HALF):
             nc.vector.transpose(wgt_t[:, lo : lo + HALF], wgt_wide[:, lo : lo + HALF])
+
+        window0 = held.tile([P, T], F32, name="window0", tag="wide_then_window", align_bytes=64)
+        nc.gpsimd.memset(window0[:], 0.0)
+        windows = [window0, window1]
 
         nc.tensor.transpose(bias_turned[:], bias_rows[:], identity[:])
         nc.scalar.copy(bias[:], bias_turned[:, 0 : M // P])

@@ -37,8 +37,8 @@ def tile_list_hboth_bias_kernel(
 
         lists_in = held.tile([P, S // 16], U16, name="lists_in")
         lists_out = held.tile([P, S // 16], U16, name="lists_out")
-        picks = held.tile([P, 18 * N_MM], F32, name="picks")
-        wgt_t = held.tile([P, S], F32, name="wgt_t", align_bytes=64)
+        picks = held.tile([P, 21 * N_MM], F32, name="picks", align_bytes=64)
+        wgt_t = picks[:, 17 * N_MM :]
         wgt_runs = held.tile([P, BLOCK], F32, name="wgt_runs", align_bytes=64)
         wgt_turned = held.tile([P, BLOCK], F32, name="wgt_turned", align_bytes=64)
         wgt_wide = held.tile([P, S], F32, name="wgt_wide", tag="wide_then_window", align_bytes=64)
@@ -163,11 +163,16 @@ def tile_list_hboth_bias_kernel(
             nc.scalar.copy(grouped[:, lo:hi, 0:2], by_plane[:, lo:hi, 0:2])
         gather(11, 2, 0, last)
         gather(15, 3, 0, N_MM)
-        gather(16, 3, N_MM, last)
-        nc.scalar.copy(grouped[:, 0:N_MM, 2:4], places[:, 11:16:4, :].rearrange("p t n -> p n t"))
+        gather(16, 3, N_MM, HALF)
+        first = places[:, 11:16:4, :].rearrange("p t n -> p n t")
+        shared = N_MM // 2
+        nc.scalar.copy(grouped[:, 0:shared, 2:4], first[:, 0:shared, :])
+        nc.vector.tensor_copy(grouped[:, shared:N_MM, 2:4], first[:, shared:N_MM, :])
+        gather(17, 3, HALF, last)
         quantize(codes0[:], 0, N_MM, grouped[:, 0:N_MM, :])
-        middle = picks[:, 10 * N_MM :].rearrange("p (t n) -> p n t", t=2)
-        nc.scalar.copy(grouped[:, N_MM:last, 2:4], middle[:, HALF:S, :])
+        middle = picks[:, 10 * N_MM : 18 * N_MM].rearrange("p (t n) -> p n t", t=2)
+        for lo in (N_MM, HALF):
+            nc.scalar.copy(grouped[:, lo : lo + N_MM, 2:4], middle[:, lo + N_MM : lo + HALF, :])
         gather(11, 2, last, S)
         gather(15, 3, last, S)
         quantize(codes1[:], N_MM, last, grouped[:, N_MM:last, :])

@@ -72,7 +72,7 @@ def tile_list_hboth_bias_kernel(
                 source[0, 4 * q : 4 * q + 4, :].bitcast(I32),
             )
 
-        nc.sync.dma_start(wgt_runs[:], wgt.rearrange("(g r) j -> g r j", r=GROUP)[:, 0, :])
+        nc.sync.dma_start(wgt_runs[:], wgt.rearrange("r (u c) -> (r u) c", u=2)[0 : 2 * P : GROUP + 1, :])
         nc.sync.dma_start(planes[0][:], x_rows[:, 0, :])
         nc.sync.dma_start(lists_in[:], offs)
         nc.sync.dma_start(bias_rows[0 : M // P, :], b.rearrange("(m p) -> m p", p=P))

@@ -157,24 +157,27 @@ def tile_list_hboth_bias_kernel(
 
         for lo in (0, HALF):
             gather(lo // N_MM, 0, lo, lo + HALF)
-        gather(4, 1, 0, S)
         last = 3 * N_MM
+        gather(4, 1, 0, last)
         for lo, hi in ((0, N_MM), (N_MM, last)):
             nc.scalar.copy(grouped[:, lo:hi, 0:2], by_plane[:, lo:hi, 0:2])
-        gather(11, 2, 0, last)
-        gather(15, 3, 0, N_MM)
-        gather(16, 3, N_MM, HALF)
-        first = places[:, 11:16:4, :].rearrange("p t n -> p n t")
+        gather(7, 2, 0, last)
+        gather(11, 3, 0, N_MM)
+        gather(15, 3, N_MM, HALF)
+
+        def pair(place2, place3):
+            return places[:, place2 : place3 + 1 : place3 - place2, :].rearrange("p t n -> p n t")
+
+        first = pair(7, 11)
         shared = N_MM // 2
         nc.scalar.copy(grouped[:, 0:shared, 2:4], first[:, 0:shared, :])
         nc.vector.tensor_copy(grouped[:, shared:N_MM, 2:4], first[:, shared:N_MM, :])
         gather(17, 3, HALF, last)
         quantize(codes0[:], 0, N_MM, grouped[:, 0:N_MM, :])
-        middle = picks[:, 10 * N_MM : 18 * N_MM].rearrange("p (t n) -> p n t", t=2)
-        for lo in (N_MM, HALF):
-            nc.scalar.copy(grouped[:, lo : lo + N_MM, 2:4], middle[:, lo + N_MM : lo + HALF, :])
-        gather(11, 2, last, S)
-        gather(15, 3, last, S)
+        nc.scalar.copy(grouped[:, N_MM:HALF, 2:4], pair(8, 15))
+        nc.scalar.copy(grouped[:, HALF:last, 2:4], pair(9, 17))
+        for t in (1, 2, 3):
+            gather(4 * t + 3, t, last, S)
         quantize(codes1[:], N_MM, last, grouped[:, N_MM:last, :])
 
         def product(m, i, rhs):

@@ -24,6 +24,7 @@ LIST_COLS = HALF // 16
 N_MM = 128
 BLOCK = 32
 GROUP = 16
+ROW_ALIGN = 256
 FLOPS = 2 * 2 * K * M * S
 
 
@@ -41,16 +42,16 @@ def tile_list_hboth_bias_kernel(
         wgt_t = picks[:, 17 * N_MM :]
         wgt_runs = held.tile([P, BLOCK], F32, name="wgt_runs", align_bytes=64)
         wgt_turned = held.tile([P, BLOCK], F32, name="wgt_turned", align_bytes=64)
-        wgt_wide = held.tile([P, S], F32, name="wgt_wide", tag="wide_then_window", align_bytes=64)
-        wgo_t = held.tile([P, S], F32, name="wgo_t")
+        wgt_wide = held.tile([P, S], F32, name="wgt_wide", tag="wide_then_window", align_bytes=ROW_ALIGN)
+        wgo_t = held.tile([P, S], F32, name="wgo_t", align_bytes=ROW_ALIGN)
         bias = held.tile([P, M // P], F32, name="bias")
         bias_rows = held.tile([P, P], F32, name="bias_rows", align_bytes=64)
         identity = held.tile([P, P], F32, name="identity", align_bytes=64)
-        planes = [held.tile([P, T], F32, name=f"plane{t}") for t in range(PACK)]
-        w4 = held.tile([P, 2 * M], U8, name="w4", align_bytes=64)
-        r8 = held.tile([P, 4 * M], U8, name="r8", align_bytes=64)
+        planes = [held.tile([P, T], F32, name=f"plane{t}", align_bytes=ROW_ALIGN) for t in range(PACK)]
+        w4 = held.tile([P, 2 * M], U8, name="w4", align_bytes=ROW_ALIGN)
+        r8 = held.tile([P, 4 * M], U8, name="r8", align_bytes=ROW_ALIGN)
         scales = held.tile([P, 2 * M], U8, name="scales", align_bytes=64)
-        window1 = held.tile([P, T], F32, name="window1")
+        window1 = held.tile([P, T], F32, name="window1", align_bytes=ROW_ALIGN)
         grouped = held.tile([P, 3 * N_MM, PACK], BF16, name="grouped", align_bytes=64)
         codes0 = held.tile([P, N_MM], U32, name="codes0", tag="first_codes", align_bytes=64)
         codes1 = held.tile([P, HALF], U32, name="codes1", align_bytes=64)
@@ -100,7 +101,7 @@ def tile_list_hboth_bias_kernel(
         for lo in (0, HALF):
             nc.vector.transpose(wgt_t[:, lo : lo + HALF], wgt_wide[:, lo : lo + HALF])
 
-        window0 = held.tile([P, T], F32, name="window0", tag="wide_then_window", align_bytes=64)
+        window0 = held.tile([P, T], F32, name="window0", tag="wide_then_window", align_bytes=ROW_ALIGN)
         nc.gpsimd.memset(window0[:], 0.0)
         windows = [window0, window1]
 

@@ -76,10 +76,10 @@ def tile_list_hboth_bias_kernel(
         nc.sync.dma_start(wgt_runs[:], wgt.rearrange("r (u c) -> (r u) c", u=2)[0 : 2 * P : GROUP + 1, :])
         nc.sync.dma_start(planes[0][:], x_rows[:, 0, :])
         nc.sync.dma_start(lists_in[:], offs)
+        nc.sync.dma_start(planes[1][:], x_rows[:, 1, :])
         nc.sync.dma_start(bias_rows[0 : M // P, :], b.rearrange("(m p) -> m p", p=P))
         for q in range(2):
             load_scales(nc.sync, w4_scales, q, 0)
-        nc.sync.dma_start(planes[1][:], x_rows[:, 1, :])
         load_scales(nc.sync, w4_scales, 3, 0)
         nc.sync.dma_start(planes[2][:], x_rows[:, 2, :])
         nc.sync.dma_start(planes[3][:], x_rows[:, 3, :])

from contextlib import ExitStack

import concourse.mybir as mybir
from concourse.masks import make_identity

K, M, T, S = 512, 256, 1024, 512

F32 = mybir.dt.float32
BF16 = mybir.dt.bfloat16
I32 = mybir.dt.int32
U32 = mybir.dt.uint32
U16 = mybir.dt.uint16
U8 = mybir.dt.uint8
E4M3X4 = mybir.dt.float8_e4m3fn_x4
E2M1X4 = mybir.dt.float4_e2m1fn_x4
MULT = mybir.AluOpType.mult
COPY = mybir.ActivationFunctionType.Copy
IDENTITY = mybir.ActivationFunctionType.Identity

P = 128
PACK = 4
HALF = S // 2
LIST_COLS = HALF // 16
N_MM = 128
BLOCK = 32
GROUP = 16
ROW_ALIGN = 256
FLOPS = 2 * 2 * K * M * S


def tile_list_hboth_bias_kernel(
    tc, xT, w4_words, w4_scales, r8_words, r8_scales, wgt, b, wgo, offs, offs2, out
):
    nc = tc.nc
    with ExitStack() as ctx:
        held = ctx.enter_context(tc.tile_pool(name="held", bufs=1))
        psum = ctx.enter_context(tc.psum_pool(name="psum", bufs=1))

        lists_in = held.tile([P, S // 16], U16, name="lists_in")
        lists_out = held.tile([P, S // 16], U16, name="lists_out")
        picks = held.tile([P, 21 * N_MM], F32, name="picks", align_bytes=64)
        wgt_t = picks[:, 17 * N_MM :]
        wgt_runs = held.tile([P, BLOCK], F32, name="wgt_runs", align_bytes=64)
        wgt_turned = held.tile([P, BLOCK], F32, name="wgt_turned", align_bytes=64)
        wgt_wide = held.tile([P, S], F32, name="wgt_wide", tag="wide_then_window", align_bytes=ROW_ALIGN)
        wgo_t = held.tile([P, S], F32, name="wgo_t", align_bytes=ROW_ALIGN)
        bias = held.tile([P, M // P], F32, name="bias")
        bias_rows = held.tile([P, P], F32, name="bias_rows", align_bytes=64)
        identity = held.tile([P, P], F32, name="identity", align_bytes=64)
        planes = [held.tile([P, T], F32, name=f"plane{t}", align_bytes=ROW_ALIGN) for t in range(PACK)]
        w4 = held.tile([P, 2 * M], U8, name="w4", align_bytes=ROW_ALIGN)
        r8 = held.tile([P, 4 * M], U8, name="r8", align_bytes=ROW_ALIGN)
        scales = held.tile([P, 2 * M], U8, name="scales", align_bytes=64)
        window1 = held.tile([P, T], F32, name="window1", align_bytes=ROW_ALIGN)
        grouped = held.tile([P, 3 * N_MM, PACK], BF16, name="grouped", align_bytes=64)
        codes0 = held.tile([P, N_MM], U32, name="codes0", tag="first_codes", align_bytes=64)
        codes1 = held.tile([P, HALF], U32, name="codes1", align_bytes=64)
        y_first = held.tile([P, N_MM], F32, name="y_first", tag="first_y", align_bytes=64)
        xscales = held.tile([P, S], U8, name="xscales", align_bytes=64)
        y = [held.tile([P, S], F32, name=f"y{m}") for m in range(M // P)]
        bias_turned = psum.tile([P, P], F32, name="bias_turned", tag="acc03")

        nc.vector.memset(bias_rows[:], 0.0)
        nc.vector.memset(scales[:].bitcast(I32), 0)
        make_identity(nc, identity[:])
        nc.vector.memset(window1[:].bitcast(I32), 0)

        x_rows = xT.rearrange("(p j) w -> p j w", j=PACK)

        def load_scales(queue, source, q, first):
            queue.dma_start(
                scales[32 * q : 32 * q + 4, first : first + M].bitcast(I32),
                source[0, 4 * q : 4 * q + 4, :].bitcast(I32),
            )

        nc.sync.dma_start(wgt_runs[:], wgt.rearrange("r (u c) -> (r u) c", u=2)[0 : 2 * P : GROUP + 1, :])
        nc.sync.dma_start(planes[0][:], x_rows[:, 0, :])
        nc.sync.dma_start(lists_in[:], offs)
        nc.sync.dma_start(planes[1][:], x_rows[:, 1, :])
        nc.sync.dma_start(bias_rows[0 : M // P, :], b.rearrange("(m p) -> m p", p=P))
        for q in range(2):
            load_scales(nc.sync, w4_scales, q, 0)
        load_scales(nc.sync, w4_scales, 3, 0)
        nc.sync.dma_start(planes[2][:], x_rows[:, 2, :])
        nc.sync.dma_start(planes[3][:], x_rows[:, 3, :])
        nc.sync.dma_start(r8[:].bitcast(I32), r8_words[0].rearrange("p n i -> p (n i)").bitcast(I32))
        load_scales(nc.sync, w4_scales, 2, 0)
        for q in range(4):
            load_scales(nc.sync, r8_scales, q, M)
        nc.sync.dma_start(w4[:].bitcast(I32), w4_words[0].bitcast(I32))
        nc.sync.dma_start(wgo_t[:], wgo)
        nc.sync.dma_start(lists_out[:], offs2)

        nc.vector.transpose(wgt_turned[:], wgt_runs[:])
        turned = wgt_turned[:].rearrange("p (h k) -> p k h", h=2)
        for lo in (0, HALF):
            nc.vector.tensor_copy(
                wgt_wide[:, lo : lo + HALF].rearrange("p (k h r) -> p k h r", h=2, r=GROUP),
                turned[:, lo // BLOCK : (lo + HALF) // BLOCK, :].unsqueeze(3).to_broadcast([P, HALF // BLOCK, 2, GROUP]),
            )
        for lo in (0, HALF):
            nc.vector.transpose(wgt_t[:, lo : lo + HALF], wgt_wide[:, lo : lo + HALF])

        window0 = held.tile([P, T], F32, name="window0", tag="wide_then_window", align_bytes=ROW_ALIGN)
        nc.gpsimd.memset(window0[:], 0.0)
        windows = [window0, window1]

        nc.tensor.transpose(bias_turned[:], bias_rows[:], identity[:])
        nc.scalar.copy(bias[:], bias_turned[:, 0 : M // P])
        acc = [[psum.tile([P, N_MM], F32, name=f"acc{m}{i}", tag=f"acc{m}{i}") for i in range(S // N_MM)] for m in range(M // P)]

        def gather(place, t, lo, hi):
            nc.vector.tensor_tensor(
                picks[:, place * N_MM : place * N_MM + hi - lo],
                planes[t][:].indirect(lists_in[:, lo // 16 : hi // 16]),
                wgt_t[:, lo:hi],
                MULT,
            )

        places = picks[:].rearrange("p (i n) -> p i n", n=N_MM)
        by_plane = picks[:, 0 : PACK * S].rearrange("p (t n) -> p n t", t=PACK)

        def quantize(dst, lo, hi, src):
            nc.vector.quantize_mx(
                out=dst.bitcast(E4M3X4), scales=xscales[:, lo:hi], in_=src.rearrange("p n t -> p (n t)")
            )

        def multiply(dst, m, rhs, lo):
            nc.tensor.matmul_mx(
                out=dst,
                lhsT=w4[:, 2 * m * P : 2 * (m + 1) * P].bitcast(E2M1X4),
                lhsT_scale=scales[:, m * P : (m + 1) * P],
                rhs=rhs.bitcast(E4M3X4),
                rhs_scale=xscales[:, lo : lo + N_MM],
                start=True,
                stop=False,
            )
            nc.tensor.matmul_mx(
                out=dst,
                lhsT=r8[:, 4 * m * P : 4 * (m + 1) * P].bitcast(E4M3X4),
                lhsT_scale=scales[:, M + m * P : M + (m + 1) * P],
                rhs=rhs.bitcast(E4M3X4),
                rhs_scale=xscales[:, lo : lo + N_MM],
                start=False,
                stop=True,
            )

        def sums(m, lo, hi):
            return y_first[:] if (m, lo) == (1, 0) else y[m][:, lo:hi]

        def add_bias(m, i, lo, hi):
            nc.scalar.activation(sums(m, lo, hi), acc[m][i][:], IDENTITY, bias=bias[:, m : m + 1], scale=1.0)

        def scatter(m, lo, hi):
            nc.vector.tensor_tensor(
                windows[m][:].indirect(lists_out[:, lo // 16 : hi // 16]), sums(m, lo, hi), wgo_t[:, lo:hi], MULT
            )

        for lo in (0, HALF):
            gather(lo // N_MM, 0, lo, lo + HALF)
        last = 3 * N_MM
        gather(4, 1, 0, last)
        for lo, hi in ((0, N_MM), (N_MM, last)):
            nc.scalar.copy(grouped[:, lo:hi, 0:2], by_plane[:, lo:hi, 0:2])
        gather(7, 2, 0, last)
        gather(11, 3, 0, N_MM)
        gather(15, 3, N_MM, HALF)

        def pair(place2, place3):
            return places[:, place2 : place3 + 1 : place3 - place2, :].rearrange("p t n -> p n t")

        first = pair(7, 11)
        shared = N_MM // 2
        nc.scalar.copy(grouped[:, 0:shared, 2:4], first[:, 0:shared, :])
        nc.vector.tensor_copy(grouped[:, shared:N_MM, 2:4], first[:, shared:N_MM, :])
        gather(17, 3, HALF, last)
        quantize(codes0[:], 0, N_MM, grouped[:, 0:N_MM, :])
        nc.scalar.copy(grouped[:, N_MM:HALF, 2:4], pair(8, 15))
        nc.scalar.copy(grouped[:, HALF:last, 2:4], pair(9, 17))
        for t in (1, 2, 3):
            gather(4 * t + 3, t, last, S)
        quantize(codes1[:], N_MM, last, grouped[:, N_MM:last, :])

        def product(m, i, rhs):
            multiply(acc[m][i][:], m, rhs, i * N_MM)
            add_bias(m, i, i * N_MM, (i + 1) * N_MM)

        for m in (1, 0):
            product(m, 0, codes0[:])
        for m in (1, 0):
            scatter(m, 0, N_MM)
        grouped_late = held.tile([P, N_MM, PACK], BF16, name="grouped_late", tag="first_codes", align_bytes=64)
        nc.scalar.copy(grouped_late[:], by_plane[:, last:S, :])
        codes_late = held.tile([P, N_MM], U32, name="codes_late", tag="first_y", align_bytes=64)
        quantize(codes_late[:], last, S, grouped_late[:])
        for m in (1, 0):
            for i in (1, 2):
                product(m, i, codes1[:, (i - 1) * N_MM : i * N_MM])
        scatter(1, N_MM, last)
        scatter(0, N_MM, HALF)
        for m in (1, 0):
            product(m, 3, codes_late[:])
        for m, lo in ((1, last), (0, HALF)):
            scatter(m, lo, S)
            nc.scalar.dma_start(out[m * P : (m + 1) * P, :], windows[m][:])
